import numpy as np
import ml_dtypes


def mxq(x, axis, fmt="e4m3"):
    dtype, down = {"e4m3": (ml_dtypes.float8_e4m3fn, 7), "e5m2": (ml_dtypes.float8_e5m2, 14)}[fmt]
    v = np.moveaxis(np.asarray(x, np.float32).astype(ml_dtypes.bfloat16).astype(np.float64), axis, -1)
    blocks = v.reshape(v.shape[:-1] + (-1, 32))
    amax = np.abs(blocks).max(-1, keepdims=True)
    byte = np.maximum(np.where(amax > 0, np.frexp(amax)[1] - 1 + 127, 0) - down, 1)
    scale = np.exp2(byte - 127.0)
    codes = (blocks / scale).astype(np.float32).astype(dtype).astype(np.float64)
    return np.moveaxis((codes * scale).reshape(v.shape), -1, axis)


WIDE = False


def mx_kscale(k):
    if not WIDE:
        return np.ones(k)
    levels = np.array([10, -10, 5, -5, 0])
    if k % 512:
        return np.exp2(np.random.permutation(np.resize(levels, k // 32))).repeat(32)
    a = np.empty((k // 512, 16))
    for p in range(k // 512):
        a[p, :8] = np.random.permutation(np.resize(levels, 8))
        for g in range(8):
            far = levels[np.abs(levels - a[p, g]) >= 10]
            a[p, g + 8] = far[np.random.randint(len(far))]
    return np.exp2(a.ravel()).repeat(32)


def f64(x):
    return np.asarray(x).astype(np.float64)


def striped(idx):
    return np.tile(np.asarray(idx).reshape(-1, 16).T, (8, 1)).astype(np.uint16)


def unstriped(offs):
    return offs[:16].T.reshape(-1).astype(np.int64)


E2M1 = np.array([0.0, 0.5, 1.0, 1.5, 2.0, 3.0, 4.0, 6.0, -0.0, -0.5, -1.0, -1.5, -2.0, -3.0, -4.0, -6.0])


def pack_weight(w, fmt):
    k, n = w.shape
    w = f64(np.asarray(w, np.float32).astype(ml_dtypes.bfloat16)).reshape(k // 32, 32, n)
    amax = np.abs(w).max(1)
    if fmt == "e4m3":
        byte = np.frexp(amax)[1] - 1 + 127 - 7
    else:
        mant, ex = np.frexp(amax / 6.0)
        byte = np.where(mant > 0.5, ex, ex - 1) + 127
    byte = np.clip(np.where(amax > 0, byte, 1), 1, 254)
    scaled = (w * np.exp2(127.0 - byte)[:, None, :]).reshape(k, n).astype(np.float32)
    by_word = np.ascontiguousarray(scaled.reshape(k // 512, 128, 4, n).transpose(0, 1, 3, 2))
    if fmt == "e4m3":
        words = by_word.astype(ml_dtypes.float8_e4m3fn).view(np.uint8)
    else:
        c = by_word.astype(ml_dtypes.float4_e2m1fn).view(np.uint8) & 0xF
        words = (c[..., 0::2] | (c[..., 1::2] << 4)).reshape(k // 512, 128, 2 * n)
    return np.ascontiguousarray(words), np.ascontiguousarray(byte.astype(np.uint8).reshape(k // 512, 16, n))


def unpack_weight(words, scales, fmt):
    g, _, n = scales.shape
    words = np.ascontiguousarray(words).reshape(g, 128, n, -1)
    if fmt == "e4m3":
        vals = words.view(ml_dtypes.float8_e4m3fn).astype(np.float64)
    else:
        nib = np.empty((g, 128, n, 4), np.uint8)
        nib[..., 0::2] = words & 0xF
        nib[..., 1::2] = words >> 4
        vals = E2M1[nib]
    vals = vals * np.repeat(np.exp2(scales.astype(np.float64) - 127.0), 8, axis=1)[..., None]
    return vals.transpose(0, 1, 3, 2).reshape(g * 512, n)


B, N, T, D, NQ = 1, 512, 2048, 1024, 256


def setup_inputs():
    n = np.random.standard_normal
    idx = np.random.permutation(T)[:B * N]
    s = mx_kscale(D)[:, None]
    kp = pack_weight(n((D, T)) / s, "e2m1")
    return {
        "qT": (n((B, D, NQ)) * s * (1.00 / np.sqrt(D))).astype(np.float32),
        "k_words": np.ascontiguousarray(kp[0].reshape(1, 2, 128, T, 2).transpose(0, 2, 3, 1, 4)).reshape(1, 128, T, 4),
        "k_scales": kp[1],
        "offs": striped(idx),
    }


def reference(qT, k_words, k_scales, offs):
    idx = unstriped(offs)
    pick = lambda x, which: x[:, which].reshape(x.shape[0], B, -1).transpose(1, 0, 2)
    k = unpack_weight(k_words.reshape(1, 128, T, 2, 2).transpose(0, 3, 1, 2, 4).reshape(2, 128, 2 * T), k_scales, "e2m1")
    kg = pick(k, idx)
    qq = mxq(f64(qT), 1, "e4m3")
    a = qq.transpose(0, 2, 1) @ kg
    m = np.max(a, axis=-1, keepdims=True)
    e = np.exp(a - m)
    l = np.sum(e, axis=-1, keepdims=True)
    y = e / l
    return y

@@ -1,0 +1,99 @@
+from contextlib import ExitStack
+
+import concourse.mybir as mybir
+
+T, D, NQ, N = 2048, 1024, 256, 512
+FLOPS = 2 * D * NQ * N
+
+F32 = mybir.dt.float32
+BF16 = mybir.dt.bfloat16
+I32 = mybir.dt.int32
+U32 = mybir.dt.uint32
+U16 = mybir.dt.uint16
+U8 = mybir.dt.uint8
+FP8X4 = mybir.dt.float8_e4m3fn_x4
+FP4X4 = mybir.dt.float4_e2m1fn_x4
+ACT = mybir.ActivationFunctionType
+ALU = mybir.AluOpType
+AX = mybir.AxisListType
+
+P = 128
+PACK = 4
+K_PASS = P * PACK
+PASSES = D // K_PASS
+QB = NQ // P
+
+
+def tile_attend_wts_topk_kernel(tc, qT, k_words, k_scales, offs, out):
+    nc = tc.nc
+    with ExitStack() as ctx:
+        keep = ctx.enter_context(tc.tile_pool(name="keep", bufs=1))
+        psum = ctx.enter_context(tc.psum_pool(name="psum", bufs=1))
+
+        offsets = keep.tile([P, N // 16], U16, name="offsets")
+        scale_pool = keep.tile([P, T // 4], I32, name="scale_pool", align_bytes=64)
+        word_pool = keep.tile([P, T], I32, name="word_pool", align_bytes=64)
+        q_raw = [keep.tile([P, PACK, NQ], F32, name="q_raw%d" % o, align_bytes=64) for o in range(PASSES)]
+
+        nc.vector.memset(scale_pool[:], 0)
+        nc.sync.dma_start(offsets[:], offs)
+        nc.scalar.dma_start(scale_pool[0:P:4, :], k_scales.bitcast(I32).rearrange("o f t -> f o t"))
+        nc.sync.dma_start(word_pool[:], k_words[0].rearrange("p t b -> p (t b)").bitcast(I32))
+        for o in range(PASSES):
+            nc.sync.dma_start(
+                q_raw[o][:], qT[0, o * K_PASS : (o + 1) * K_PASS, :].rearrange("(p j) w -> p j w", j=PACK)
+            )
+
+        k_planes = keep.tile([P, PASSES * N // 4], I32, name="k_planes", align_bytes=64)
+        nc.vector.memset(k_planes[:], 0)
+        scale_rows = keep.tile([P, N], U8, name="scale_rows", align_bytes=64)
+        nc.vector.tensor_copy(scale_rows[:], scale_pool[:].bitcast(U8).indirect(offsets[:]))
+        for q in range(4):
+            nc.scalar.dma_start(k_planes[32 * q : 32 * q + 4, :], scale_rows[32 * q : 32 * q + 32 : 4, :].bitcast(I32))
+        k_plane = [k_planes[:].bitcast(U8)[:, o * N : (o + 1) * N] for o in range(PASSES)]
+
+        word_pairs = keep.tile([P, N], U32, name="word_pairs", align_bytes=64)
+        nc.vector.tensor_copy(word_pairs[:], word_pool[:].bitcast(U32).indirect(offsets[:]))
+        halves = word_pairs[:].bitcast(U16).rearrange("p (n o) -> p o n", o=PASSES)
+        k_codes = [keep.tile([P, N], U16, name="k_codes%d" % o, align_bytes=64) for o in range(PASSES)]
+        for o in range(PASSES):
+            nc.vector.tensor_copy(k_codes[o][:], halves[:, o, :])
+
+        scores = [psum.tile([P, N], F32, name="scores%d" % b) for b in range(QB)]
+        for o in range(PASSES):
+            grouped = [keep.tile([P, P, PACK], BF16, name="grouped%d_%d" % (o, b), align_bytes=64) for b in range(QB)]
+            for b in range(QB):
+                dst = grouped[b][:].rearrange("p (c i) t -> p c t i", i=4)
+                src = q_raw[o][:, :, b * P : (b + 1) * P].rearrange("p t (c i) -> p c t i", i=4)
+                if o != b:
+                    nc.vector.tensor_copy(dst, src)
+                else:
+                    nc.scalar.activation(dst, src, ACT.Copy)
+            for b in range(QB):
+                q_codes = keep.tile([P, P], U32, name="q_codes%d_%d" % (o, b), align_bytes=64)
+                q_plane = keep.tile([P, P], U8, name="q_plane%d_%d" % (o, b), align_bytes=64)
+                nc.vector.quantize_mx(
+                    out=q_codes[:].bitcast(FP8X4), scales=q_plane[:], in_=grouped[b][:].rearrange("p w j -> p (w j)")
+                )
+                nc.tensor.matmul_mx(
+                    out=scores[b][:],
+                    lhsT=q_codes[:].bitcast(FP8X4),
+                    lhsT_scale=q_plane[:],
+                    rhs=k_codes[o][:].bitcast(FP4X4),
+                    rhs_scale=k_plane[o],
+                    start=(o == 0),
+                    stop=(o == PASSES - 1),
+                )
+
+        neg_max = [keep.tile([P, 1], F32, name="neg_max%d" % b) for b in range(QB)]
+        row_sum = [keep.tile([P, 1], F32, name="row_sum%d" % b) for b in range(QB)]
+        e = [keep.tile([P, N], F32, name="e%d" % b) for b in range(QB)]
+        for b in range(QB):
+            nc.vector.tensor_reduce(neg_max[b][:], scores[b][:], AX.X, ALU.max, negate=True)
+            nc.scalar.activation(e[b][:], scores[b][:], ACT.Exp, bias=neg_max[b][:], scale=1.0, accum_out=row_sum[b][:])
+        for b in range(QB):
+            inv = keep.tile([P, 1], F32, name="inv%d" % b)
+            y = keep.tile([P, N], F32, name="y%d" % b)
+            nc.vector.reciprocal(inv[:], row_sum[b][:])
+            nc.vector.tensor_scalar(y[:], e[b][:], inv[:], None, ALU.mult)
+            nc.sync.dma_start(out[0, b * P : (b + 1) * P, :], y[:])

@@ -33,47 +33,48 @@ def tile_attend_wts_topk_kernel(tc, qT, k_words, k_scales, offs, out):
         offsets = keep.tile([P, N // 16], U16, name="offsets")
         scale_pool = keep.tile([P, T // 4], I32, name="scale_pool", align_bytes=64)
         word_pool = keep.tile([P, T], I32, name="word_pool", align_bytes=64)
-        q_raw = [keep.tile([P, PACK, NQ], F32, name="q_raw%d" % o, align_bytes=64) for o in range(PASSES)]
+        q_first = keep.tile([P, PACK, NQ], F32, name="q_first", align_bytes=64)
+        q_second0 = keep.tile([P, PACK, P], F32, name="q_second0", align_bytes=64)
+        q_rows = [qT[0, o * K_PASS : (o + 1) * K_PASS, :].rearrange("(p j) w -> p j w", j=PACK) for o in range(PASSES)]
 
-        nc.vector.memset(scale_pool[:], 0)
+        nc.vector.memset(scale_pool[0:96, :], 0)
         nc.sync.dma_start(offsets[:], offs)
-        nc.scalar.dma_start(scale_pool[0:P:4, :], k_scales.bitcast(I32).rearrange("o f t -> f o t"))
+        nc.sync.dma_start(scale_pool[96:P, :], k_scales.bitcast(I32).rearrange("o f t -> f o t"))
         nc.sync.dma_start(word_pool[:], k_words[0].rearrange("p t b -> p (t b)").bitcast(I32))
-        for o in range(PASSES):
-            nc.sync.dma_start(
-                q_raw[o][:], qT[0, o * K_PASS : (o + 1) * K_PASS, :].rearrange("(p j) w -> p j w", j=PACK)
-            )
+        nc.sync.dma_start(q_first[:], q_rows[0])
+        nc.sync.dma_start(q_second0[:], q_rows[1][:, :, 0:P])
 
         k_planes = keep.tile([P, PASSES * N // 4], I32, name="k_planes", align_bytes=64)
         nc.vector.memset(k_planes[:], 0)
         scale_rows = keep.tile([P, N], U8, name="scale_rows", align_bytes=64)
         nc.vector.tensor_copy(scale_rows[:], scale_pool[:].bitcast(U8).indirect(offsets[:]))
         for q in range(4):
-            nc.scalar.dma_start(k_planes[32 * q : 32 * q + 4, :], scale_rows[32 * q : 32 * q + 32 : 4, :].bitcast(I32))
+            nc.sync.dma_start(k_planes[32 * q : 32 * q + 4, :], scale_rows[96 + 8 * q : 96 + 8 * q + 8, :].bitcast(I32))
+        q_second1 = keep.tile([P, PACK, P], F32, name="q_second1", align_bytes=64)
+        nc.sync.dma_start(q_second1[:], q_rows[1][:, :, P:NQ])
+        q_raw = [[q_first[:, :, 0:P], q_first[:, :, P:NQ]], [q_second0[:], q_second1[:]]]
         k_plane = [k_planes[:].bitcast(U8)[:, o * N : (o + 1) * N] for o in range(PASSES)]
 
         word_pairs = keep.tile([P, N], U32, name="word_pairs", align_bytes=64)
         nc.vector.tensor_copy(word_pairs[:], word_pool[:].bitcast(U32).indirect(offsets[:]))
         halves = word_pairs[:].bitcast(U16).rearrange("p (n o) -> p o n", o=PASSES)
         k_codes = [keep.tile([P, N], U16, name="k_codes%d" % o, align_bytes=64) for o in range(PASSES)]
-        for o in range(PASSES):
-            nc.vector.tensor_copy(k_codes[o][:], halves[:, o, :])
 
         scores = [psum.tile([P, N], F32, name="scores%d" % b) for b in range(QB)]
         for o in range(PASSES):
-            grouped = [keep.tile([P, P, PACK], BF16, name="grouped%d_%d" % (o, b), align_bytes=64) for b in range(QB)]
-            for b in range(QB):
-                dst = grouped[b][:].rearrange("p (c i) t -> p c t i", i=4)
-                src = q_raw[o][:, :, b * P : (b + 1) * P].rearrange("p t (c i) -> p c t i", i=4)
-                if o != b:
-                    nc.vector.tensor_copy(dst, src)
-                else:
-                    nc.scalar.activation(dst, src, ACT.Copy)
-            for b in range(QB):
+            nc.vector.tensor_copy(k_codes[o][:], halves[:, o, :])
+        for b in range(QB):
+            for o in range(PASSES):
+                grouped = keep.tile(
+                    [P, P, PACK], BF16, name="grouped%d_%d" % (o, b), tag="grouped%d_%d" % (o, b), align_bytes=64
+                )
+                dst = grouped[:].rearrange("p (c i) t -> p c t i", i=4)
+                src = q_raw[o][b].rearrange("p t (c i) -> p c t i", i=4)
+                nc.scalar.activation(dst, src, ACT.Copy)
                 q_codes = keep.tile([P, P], U32, name="q_codes%d_%d" % (o, b), align_bytes=64)
                 q_plane = keep.tile([P, P], U8, name="q_plane%d_%d" % (o, b), align_bytes=64)
                 nc.vector.quantize_mx(
-                    out=q_codes[:].bitcast(FP8X4), scales=q_plane[:], in_=grouped[b][:].rearrange("p w j -> p (w j)")
+                    out=q_codes[:].bitcast(FP8X4), scales=q_plane[:], in_=grouped[:].rearrange("p w j -> p (w j)")
                 )
                 nc.tensor.matmul_mx(
                     out=scores[b][:],
@@ -85,7 +86,9 @@ def tile_attend_wts_topk_kernel(tc, qT, k_words, k_scales, offs, out):
                     stop=(o == PASSES - 1),
                 )
 
-        neg_max = [keep.tile([P, 1], F32, name="neg_max%d" % b) for b in range(QB)]
+        neg_max = [
+            keep.tile([P, 1], F32, name="neg_max%d" % b, tag="grouped1_%d" % (1 - b), align_bytes=64) for b in range(QB)
+        ]
         row_sum = [keep.tile([P, 1], F32, name="row_sum%d" % b) for b in range(QB)]
         e = [keep.tile([P, N], F32, name="e%d" % b) for b in range(QB)]
         for b in range(QB):

@@ -1,6 +1,7 @@
 from contextlib import ExitStack
 
 import concourse.mybir as mybir
+from concourse.masks import make_identity
 
 T, D, NQ, N = 2048, 1024, 256, 512
 FLOPS = 2 * D * NQ * N
@@ -44,6 +45,13 @@ def tile_attend_wts_topk_kernel(tc, qT, k_words, k_scales, offs, out):
         nc.sync.dma_start(q_first[:], q_rows[0])
         nc.sync.dma_start(q_second0[:], q_rows[1][:, :, 0:P])
 
+        ident = keep.tile([P, P], BF16, name="ident", align_bytes=64)
+        make_identity(nc, ident[:])
+        warm = [psum.tile([P, 8 * P], BF16, name="warm%d" % i) for i in range(4)]
+        for i in range(64):
+            j = (i // 4) % 8
+            nc.tensor.transpose(warm[i % 4][:, j * P : (j + 1) * P], ident[:], ident[:])
+
         k_planes = keep.tile([P, PASSES * N // 4], I32, name="k_planes", align_bytes=64)
         nc.vector.memset(k_planes[:], 0)
         scale_rows = keep.tile([P, N], U8, name="scale_rows", align_bytes=64)
@@ -66,11 +74,14 @@ def tile_attend_wts_topk_kernel(tc, qT, k_words, k_scales, offs, out):
         for b in range(QB):
             for o in range(PASSES):
                 grouped = keep.tile(
-                    [P, P, PACK], BF16, name="grouped%d_%d" % (o, b), tag="grouped%d_%d" % (o, b), align_bytes=64
+                    [P, P, PACK], BF16, name="grouped%d_%d" % (o, b), tag="grouped%d_%d" % (o, b * o), align_bytes=64
                 )
                 dst = grouped[:].rearrange("p (c i) t -> p c t i", i=4)
                 src = q_raw[o][b].rearrange("p t (c i) -> p c t i", i=4)
-                nc.scalar.activation(dst, src, ACT.Copy)
+                if (o, b) == (0, 1):
+                    nc.vector.tensor_copy(dst, src)
+                else:
+                    nc.scalar.activation(dst, src, ACT.Copy)
                 q_codes = keep.tile([P, P], U32, name="q_codes%d_%d" % (o, b), align_bytes=64)
                 q_plane = keep.tile([P, P], U8, name="q_plane%d_%d" % (o, b), align_bytes=64)
                 nc.vector.quantize_mx(
@@ -96,7 +107,13 @@ def tile_attend_wts_topk_kernel(tc, qT, k_words, k_scales, offs, out):
             nc.scalar.activation(e[b][:], scores[b][:], ACT.Exp, bias=neg_max[b][:], scale=1.0, accum_out=row_sum[b][:])
         for b in range(QB):
             inv = keep.tile([P, 1], F32, name="inv%d" % b)
-            y = keep.tile([P, N], F32, name="y%d" % b)
             nc.vector.reciprocal(inv[:], row_sum[b][:])
-            nc.vector.tensor_scalar(y[:], e[b][:], inv[:], None, ALU.mult)
-            nc.sync.dma_start(out[0, b * P : (b + 1) * P, :], y[:])
+            rows = out[0, b * P : (b + 1) * P, :]
+            cut = N if b == 0 else 320
+            y = keep.tile([P, cut], F32, name="y%d" % b)
+            nc.vector.tensor_scalar(y[:], e[b][:, 0:cut], inv[:], None, ALU.mult)
+            nc.sync.dma_start(rows[:, 0:cut], y[:])
+            if cut < N:
+                y_rest = keep.tile([P, N - cut], F32, name="y_rest")
+                nc.scalar.activation(y_rest[:], e[b][:, cut:N], ACT.Copy, scale=inv[:])
+                nc.scalar.dma_start(rows[:, cut:N], y_rest[:])

@@ -1,7 +1,6 @@
 from contextlib import ExitStack
 
 import concourse.mybir as mybir
-from concourse.masks import make_identity
 
 T, D, NQ, N = 2048, 1024, 256, 512
 FLOPS = 2 * D * NQ * N
@@ -34,23 +33,16 @@ def tile_attend_wts_topk_kernel(tc, qT, k_words, k_scales, offs, out):
         offsets = keep.tile([P, N // 16], U16, name="offsets")
         scale_pool = keep.tile([P, T // 4], I32, name="scale_pool", align_bytes=64)
         word_pool = keep.tile([P, T], I32, name="word_pool", align_bytes=64)
-        q_first = keep.tile([P, PACK, NQ], F32, name="q_first", align_bytes=64)
-        q_second0 = keep.tile([P, PACK, P], F32, name="q_second0", align_bytes=64)
         q_rows = [qT[0, o * K_PASS : (o + 1) * K_PASS, :].rearrange("(p j) w -> p j w", j=PACK) for o in range(PASSES)]
 
         nc.vector.memset(scale_pool[0:96, :], 0)
         nc.sync.dma_start(offsets[:], offs)
         nc.sync.dma_start(scale_pool[96:P, :], k_scales.bitcast(I32).rearrange("o f t -> f o t"))
         nc.sync.dma_start(word_pool[:], k_words[0].rearrange("p t b -> p (t b)").bitcast(I32))
-        nc.sync.dma_start(q_first[:], q_rows[0])
-        nc.sync.dma_start(q_second0[:], q_rows[1][:, :, 0:P])
-
-        ident = keep.tile([P, P], BF16, name="ident", align_bytes=64)
-        make_identity(nc, ident[:])
-        warm = [psum.tile([P, 8 * P], BF16, name="warm%d" % i) for i in range(4)]
-        for i in range(64):
-            j = (i // 4) % 8
-            nc.tensor.transpose(warm[i % 4][:, j * P : (j + 1) * P], ident[:], ident[:])
+        q_tile = [[keep.tile([P, PACK, P], F32, name="q_raw%d_%d" % (o, b), align_bytes=64) for b in range(QB)] for o in range(PASSES)]
+        q_raw = [[q_tile[o][b][:] for b in range(QB)] for o in range(PASSES)]
+        for o in range(PASSES):
+            nc.sync.dma_start(q_raw[o][0], q_rows[o][:, :, 0:P])
 
         k_planes = keep.tile([P, PASSES * N // 4], I32, name="k_planes", align_bytes=64)
         nc.vector.memset(k_planes[:], 0)
@@ -58,48 +50,61 @@ def tile_attend_wts_topk_kernel(tc, qT, k_words, k_scales, offs, out):
         nc.vector.tensor_copy(scale_rows[:], scale_pool[:].bitcast(U8).indirect(offsets[:]))
         for q in range(4):
             nc.sync.dma_start(k_planes[32 * q : 32 * q + 4, :], scale_rows[96 + 8 * q : 96 + 8 * q + 8, :].bitcast(I32))
-        q_second1 = keep.tile([P, PACK, P], F32, name="q_second1", align_bytes=64)
-        nc.sync.dma_start(q_second1[:], q_rows[1][:, :, P:NQ])
-        q_raw = [[q_first[:, :, 0:P], q_first[:, :, P:NQ]], [q_second0[:], q_second1[:]]]
+        for o in range(PASSES):
+            nc.sync.dma_start(q_raw[o][1], q_rows[o][:, :, P:NQ])
         k_plane = [k_planes[:].bitcast(U8)[:, o * N : (o + 1) * N] for o in range(PASSES)]
 
         word_pairs = keep.tile([P, N], U32, name="word_pairs", align_bytes=64)
         nc.vector.tensor_copy(word_pairs[:], word_pool[:].bitcast(U32).indirect(offsets[:]))
         halves = word_pairs[:].bitcast(U16).rearrange("p (n o) -> p o n", o=PASSES)
-        k_codes = [keep.tile([P, N], U16, name="k_codes%d" % o, align_bytes=64) for o in range(PASSES)]
-
         scores = [psum.tile([P, N], F32, name="scores%d" % b) for b in range(QB)]
-        for o in range(PASSES):
-            nc.vector.tensor_copy(k_codes[o][:], halves[:, o, :])
-        for b in range(QB):
-            for o in range(PASSES):
-                grouped = keep.tile(
-                    [P, P, PACK], BF16, name="grouped%d_%d" % (o, b), tag="grouped%d_%d" % (o, b * o), align_bytes=64
-                )
-                dst = grouped[:].rearrange("p (c i) t -> p c t i", i=4)
-                src = q_raw[o][b].rearrange("p t (c i) -> p c t i", i=4)
-                if (o, b) == (0, 1):
-                    nc.vector.tensor_copy(dst, src)
-                else:
-                    nc.scalar.activation(dst, src, ACT.Copy)
-                q_codes = keep.tile([P, P], U32, name="q_codes%d_%d" % (o, b), align_bytes=64)
-                q_plane = keep.tile([P, P], U8, name="q_plane%d_%d" % (o, b), align_bytes=64)
-                nc.vector.quantize_mx(
-                    out=q_codes[:].bitcast(FP8X4), scales=q_plane[:], in_=grouped[:].rearrange("p w j -> p (w j)")
-                )
-                nc.tensor.matmul_mx(
-                    out=scores[b][:],
-                    lhsT=q_codes[:].bitcast(FP8X4),
-                    lhsT_scale=q_plane[:],
-                    rhs=k_codes[o][:].bitcast(FP4X4),
-                    rhs_scale=k_plane[o],
-                    start=(o == 0),
-                    stop=(o == PASSES - 1),
-                )
 
-        neg_max = [
-            keep.tile([P, 1], F32, name="neg_max%d" % b, tag="grouped1_%d" % (1 - b), align_bytes=64) for b in range(QB)
-        ]
+        def part_words(o, tag):
+            codes = keep.tile([P, N], U16, name="k_codes%d" % o, tag=tag, align_bytes=64)
+            nc.vector.tensor_copy(codes[:], halves[:, o, :])
+            return codes
+
+        def bf16_tile(o, b, tag=None):
+            return keep.tile([P, P, PACK], BF16, name="grouped%d_%d" % (o, b), tag=tag or "grouped%d_%d" % (o, b), align_bytes=64)
+
+        def round_q(grouped, o, b, lo, hi, on_vector):
+            dst = grouped[:, lo:hi, :].rearrange("p (c i) t -> p c t i", i=4)
+            src = q_raw[o][b][:, :, lo:hi].rearrange("p t (c i) -> p c t i", i=4)
+            if on_vector:
+                nc.vector.tensor_copy(dst, src)
+            else:
+                nc.scalar.activation(dst, src, ACT.Copy)
+
+        def multiply(o, b, grouped, k_codes, tag=None):
+            q_codes = keep.tile([P, P], U32, name="q_codes%d_%d" % (o, b), tag=tag or "q_codes%d_%d" % (o, b), align_bytes=64)
+            q_plane = keep.tile([P, P], U8, name="q_plane%d_%d" % (o, b), align_bytes=64)
+            nc.vector.quantize_mx(
+                out=q_codes[:].bitcast(FP8X4), scales=q_plane[:], in_=grouped[:].rearrange("p w j -> p (w j)")
+            )
+            nc.tensor.matmul_mx(
+                out=scores[b][:],
+                lhsT=q_codes[:].bitcast(FP8X4),
+                lhsT_scale=q_plane[:],
+                rhs=k_codes[:].bitcast(FP4X4),
+                rhs_scale=k_plane[o],
+                start=(o == 0),
+                stop=(o == PASSES - 1),
+            )
+
+        g00, g01, g10, g11 = bf16_tile(0, 0), bf16_tile(0, 1), bf16_tile(1, 0), bf16_tile(1, 1)
+        round_q(g00, 0, 0, 0, P, False)
+        k_first = part_words(0, "k_first")
+        multiply(0, 0, g00, k_first)
+        k_second = part_words(1, "grouped0_0")
+        round_q(g10, 1, 0, 0, P, False)
+        multiply(1, 0, g10, k_second)
+        round_q(g01, 0, 1, 0, P, False)
+        multiply(0, 1, g01, k_first)
+        round_q(g11, 1, 1, 0, 48, False)
+        round_q(g11, 1, 1, 48, P, True)
+        multiply(1, 1, g11, k_second)
+
+        neg_max = [keep.tile([P, 1], F32, name="neg_max%d" % b, tag=("grouped1_1", "neg_max1")[b], align_bytes=64) for b in range(QB)]
         row_sum = [keep.tile([P, 1], F32, name="row_sum%d" % b) for b in range(QB)]
         e = [keep.tile([P, N], F32, name="e%d" % b) for b in range(QB)]
         for b in range(QB):
@@ -109,11 +114,9 @@ def tile_attend_wts_topk_kernel(tc, qT, k_words, k_scales, offs, out):
             inv = keep.tile([P, 1], F32, name="inv%d" % b)
             nc.vector.reciprocal(inv[:], row_sum[b][:])
             rows = out[0, b * P : (b + 1) * P, :]
-            cut = N if b == 0 else 320
-            y = keep.tile([P, cut], F32, name="y%d" % b)
-            nc.vector.tensor_scalar(y[:], e[b][:, 0:cut], inv[:], None, ALU.mult)
-            nc.sync.dma_start(rows[:, 0:cut], y[:])
-            if cut < N:
-                y_rest = keep.tile([P, N - cut], F32, name="y_rest")
-                nc.scalar.activation(y_rest[:], e[b][:, cut:N], ACT.Copy, scale=inv[:])
-                nc.scalar.dma_start(rows[:, cut:N], y_rest[:])
+            parts = 1 if b == 0 else 2
+            for h in range(parts):
+                cols = slice(h * N // parts, (h + 1) * N // parts)
+                y = keep.tile([P, N // parts], F32, name="y%d_%d" % (b, h))
+                nc.vector.tensor_scalar(y[:], e[b][:, cols], inv[:], None, ALU.mult)
+                nc.sync.dma_start(rows[:, cols], y[:])

@@ -114,7 +114,7 @@ def tile_attend_wts_topk_kernel(tc, qT, k_words, k_scales, offs, out):
             inv = keep.tile([P, 1], F32, name="inv%d" % b)
             nc.vector.reciprocal(inv[:], row_sum[b][:])
             rows = out[0, b * P : (b + 1) * P, :]
-            parts = 1 if b == 0 else 2
+            parts = 2
             for h in range(parts):
                 cols = slice(h * N // parts, (h + 1) * N // parts)
                 y = keep.tile([P, N // parts], F32, name="y%d_%d" % (b, h))

@@ -98,10 +98,11 @@ def tile_attend_wts_topk_kernel(tc, qT, k_words, k_scales, offs, out):
         k_second = part_words(1, "grouped0_0")
         round_q(g10, 1, 0, 0, P, False)
         multiply(1, 0, g10, k_second)
-        round_q(g01, 0, 1, 0, P, False)
-        multiply(0, 1, g01, k_first)
+        round_q(g01, 0, 1, 0, 104, False)
+        round_q(g01, 0, 1, 104, P, True)
         round_q(g11, 1, 1, 0, 48, False)
         round_q(g11, 1, 1, 48, P, True)
+        multiply(0, 1, g01, k_first)
         multiply(1, 1, g11, k_second)
 
         neg_max = [keep.tile([P, 1], F32, name="neg_max%d" % b, tag=("grouped1_1", "neg_max1")[b], align_bytes=64) for b in range(QB)]

@@ -35,23 +35,32 @@ def tile_attend_wts_topk_kernel(tc, qT, k_words, k_scales, offs, out):
         word_pool = keep.tile([P, T], I32, name="word_pool", align_bytes=64)
         q_rows = [qT[0, o * K_PASS : (o + 1) * K_PASS, :].rearrange("(p j) w -> p j w", j=PACK) for o in range(PASSES)]
 
+        def load_q(o, lo, hi, queue=nc.sync, tag=None):
+            name = "q_raw%d_%d" % (o, lo)
+            raw = keep.tile([P, PACK, hi - lo], F32, name=name, tag=tag or name, align_bytes=64)
+            queue.dma_start(raw[:], q_rows[o][:, :, lo:hi])
+            return raw
+
         nc.vector.memset(scale_pool[0:96, :], 0)
+        nc.scalar.dma_start(scale_pool[96:P, :], k_scales.bitcast(I32).rearrange("o f t -> f o t"))
         nc.sync.dma_start(offsets[:], offs)
-        nc.sync.dma_start(scale_pool[96:P, :], k_scales.bitcast(I32).rearrange("o f t -> f o t"))
         nc.sync.dma_start(word_pool[:], k_words[0].rearrange("p t b -> p (t b)").bitcast(I32))
-        q_tile = [[keep.tile([P, PACK, P], F32, name="q_raw%d_%d" % (o, b), align_bytes=64) for b in range(QB)] for o in range(PASSES)]
-        q_raw = [[q_tile[o][b][:] for b in range(QB)] for o in range(PASSES)]
-        for o in range(PASSES):
-            nc.sync.dma_start(q_raw[o][0], q_rows[o][:, :, 0:P])
+        r00 = load_q(0, 0, P)
+        r10 = load_q(1, 0, P)
+
+        warm_in = keep.tile([P, 1], F32, name="warm_in")
+        warm_out = keep.tile([P, 1], F32, name="warm_out")
+        nc.gpsimd.memset(warm_in[:], 0.0)
+        nc.scalar.activation(warm_out[:], warm_in[:], ACT.Exp)
 
         k_planes = keep.tile([P, PASSES * N // 4], I32, name="k_planes", align_bytes=64)
         nc.vector.memset(k_planes[:], 0)
         scale_rows = keep.tile([P, N], U8, name="scale_rows", align_bytes=64)
         nc.vector.tensor_copy(scale_rows[:], scale_pool[:].bitcast(U8).indirect(offsets[:]))
         for q in range(4):
-            nc.sync.dma_start(k_planes[32 * q : 32 * q + 4, :], scale_rows[96 + 8 * q : 96 + 8 * q + 8, :].bitcast(I32))
-        for o in range(PASSES):
-            nc.sync.dma_start(q_raw[o][1], q_rows[o][:, :, P:NQ])
+            (nc.sync, nc.scalar)[q % 2].dma_start(k_planes[32 * q : 32 * q + 4, :], scale_rows[96 + 8 * q : 96 + 8 * q + 8, :].bitcast(I32))
+        r01 = load_q(0, P, NQ)
+        r11 = load_q(1, P, NQ)
         k_plane = [k_planes[:].bitcast(U8)[:, o * N : (o + 1) * N] for o in range(PASSES)]
 
         word_pairs = keep.tile([P, N], U32, name="word_pairs", align_bytes=64)
@@ -59,53 +68,75 @@ def tile_attend_wts_topk_kernel(tc, qT, k_words, k_scales, offs, out):
         halves = word_pairs[:].bitcast(U16).rearrange("p (n o) -> p o n", o=PASSES)
         scores = [psum.tile([P, N], F32, name="scores%d" % b) for b in range(QB)]
 
-        def part_words(o, tag):
-            codes = keep.tile([P, N], U16, name="k_codes%d" % o, tag=tag, align_bytes=64)
-            nc.vector.tensor_copy(codes[:], halves[:, o, :])
+        def part_words(o, lo, hi, tag=None):
+            name = "k_codes%d_%d" % (o, lo)
+            codes = keep.tile([P, hi - lo], U16, name=name, tag=tag or name, align_bytes=64)
+            nc.vector.tensor_copy(codes[:], halves[:, o, lo:hi])
             return codes
 
-        def bf16_tile(o, b, tag=None):
-            return keep.tile([P, P, PACK], BF16, name="grouped%d_%d" % (o, b), tag=tag or "grouped%d_%d" % (o, b), align_bytes=64)
+        def bf16_tile(o, b):
+            return keep.tile([P, P, PACK], BF16, name="grouped%d_%d" % (o, b), align_bytes=64)
 
-        def round_q(grouped, o, b, lo, hi, on_vector):
+        def round_q(grouped, raw, first, lo, hi, on_vector):
             dst = grouped[:, lo:hi, :].rearrange("p (c i) t -> p c t i", i=4)
-            src = q_raw[o][b][:, :, lo:hi].rearrange("p t (c i) -> p c t i", i=4)
+            src = raw[:, :, lo - first : hi - first].rearrange("p t (c i) -> p c t i", i=4)
             if on_vector:
                 nc.vector.tensor_copy(dst, src)
             else:
                 nc.scalar.activation(dst, src, ACT.Copy)
 
-        def multiply(o, b, grouped, k_codes, tag=None):
-            q_codes = keep.tile([P, P], U32, name="q_codes%d_%d" % (o, b), tag=tag or "q_codes%d_%d" % (o, b), align_bytes=64)
+        def quantise(o, b, grouped):
+            q_codes = keep.tile([P, P], U32, name="q_codes%d_%d" % (o, b), align_bytes=64)
             q_plane = keep.tile([P, P], U8, name="q_plane%d_%d" % (o, b), align_bytes=64)
             nc.vector.quantize_mx(
                 out=q_codes[:].bitcast(FP8X4), scales=q_plane[:], in_=grouped[:].rearrange("p w j -> p (w j)")
             )
+            return q_codes, q_plane
+
+        def multiply(o, b, q, k_codes, lo, hi, start, stop):
             nc.tensor.matmul_mx(
-                out=scores[b][:],
-                lhsT=q_codes[:].bitcast(FP8X4),
-                lhsT_scale=q_plane[:],
-                rhs=k_codes[:].bitcast(FP4X4),
-                rhs_scale=k_plane[o],
-                start=(o == 0),
-                stop=(o == PASSES - 1),
+                out=scores[b][:, lo:hi],
+                lhsT=q[0][:].bitcast(FP8X4),
+                lhsT_scale=q[1][:],
+                rhs=k_codes.bitcast(FP4X4),
+                rhs_scale=k_plane[o][:, lo:hi],
+                start=start,
+                stop=stop,
             )
 
-        g00, g01, g10, g11 = bf16_tile(0, 0), bf16_tile(0, 1), bf16_tile(1, 0), bf16_tile(1, 1)
-        round_q(g00, 0, 0, 0, P, False)
-        k_first = part_words(0, "k_first")
-        multiply(0, 0, g00, k_first)
-        k_second = part_words(1, "grouped0_0")
-        round_q(g10, 1, 0, 0, P, False)
-        multiply(1, 0, g10, k_second)
-        round_q(g01, 0, 1, 0, 104, False)
-        round_q(g01, 0, 1, 104, P, True)
-        round_q(g11, 1, 1, 0, 48, False)
-        round_q(g11, 1, 1, 48, P, True)
-        multiply(0, 1, g01, k_first)
-        multiply(1, 1, g11, k_second)
+        g00, g01, g10 = bf16_tile(0, 0), bf16_tile(0, 1), bf16_tile(1, 0)
+        round_q(g00, r00, 0, 0, P, False)
+        q00 = quantise(0, 0, g00)
+        k0 = keep.tile([P, N], U16, name="k_codes0", tag="q_raw0_0", align_bytes=64)
+        for lo, hi in ((0, N // 2), (N // 2, N)):
+            nc.vector.tensor_copy(k0[:, lo:hi], halves[:, 0, lo:hi])
+            multiply(0, 0, q00, k0[:, lo:hi], lo, hi, lo == 0, False)
+        k1 = part_words(1, 0, N, "grouped0_0")
+        round_q(g10, r10, 0, 0, P, False)
+        q10 = quantise(1, 0, g10)
+        multiply(1, 0, q10, k1[:], 0, N, False, True)
+        round_q(g01, r01, 0, 0, 96, False)
+        round_q(g01, r01, 0, 96, P, True)
+        q01 = quantise(0, 1, g01)
+        multiply(0, 1, q01, k0[:], 0, N, True, False)
+        q11 = (
+            keep.tile([P, P], U32, name="q_codes1_1", align_bytes=64),
+            keep.tile([P, P], U8, name="q_plane1_1", align_bytes=64),
+        )
+        g11 = [
+            keep.tile([P, 64, PACK], BF16, name="grouped1_1a", align_bytes=64),
+            keep.tile([P, 64, PACK], BF16, name="grouped1_1b", tag="grouped0_1", align_bytes=64),
+        ]
+        for h in range(2):
+            round_q(g11[h], r11, -64 * h, 0, 64, h == 1)
+        for h in range(2):
+            cols = slice(64 * h, 64 * h + 64)
+            nc.vector.quantize_mx(
+                out=q11[0][:, cols].bitcast(FP8X4), scales=q11[1][:, cols], in_=g11[h][:].rearrange("p w j -> p (w j)")
+            )
+        multiply(1, 1, q11, k1[:], 0, N, False, True)
 
-        neg_max = [keep.tile([P, 1], F32, name="neg_max%d" % b, tag=("grouped1_1", "neg_max1")[b], align_bytes=64) for b in range(QB)]
+        neg_max = [keep.tile([P, 1], F32, name="neg_max%d" % b, tag=("q_raw1_128", "neg_max1")[b], align_bytes=64) for b in range(QB)]
         row_sum = [keep.tile([P, 1], F32, name="row_sum%d" % b) for b in range(QB)]
         e = [keep.tile([P, N], F32, name="e%d" % b) for b in range(QB)]
         for b in range(QB):
@@ -115,9 +146,12 @@ def tile_attend_wts_topk_kernel(tc, qT, k_words, k_scales, offs, out):
             inv = keep.tile([P, 1], F32, name="inv%d" % b)
             nc.vector.reciprocal(inv[:], row_sum[b][:])
             rows = out[0, b * P : (b + 1) * P, :]
-            parts = 2
-            for h in range(parts):
-                cols = slice(h * N // parts, (h + 1) * N // parts)
-                y = keep.tile([P, N // parts], F32, name="y%d_%d" % (b, h))
-                nc.vector.tensor_scalar(y[:], e[b][:, cols], inv[:], None, ALU.mult)
-                nc.sync.dma_start(rows[:, cols], y[:])
+            cuts = ((0, 192), (192, N)) if b == 0 else ((0, 128), (128, 320), (320, N))
+            for lo, hi in cuts:
+                y = keep.tile([P, hi - lo], F32, name="y%d_%d" % (b, lo))
+                if b == 1 and lo == 0:
+                    nc.scalar.activation(y[:], e[b][:, lo:hi], ACT.Copy, scale=inv[:])
+                    nc.scalar.dma_start(rows[:, lo:hi], y[:])
+                else:
+                    nc.vector.tensor_scalar(y[:], e[b][:, lo:hi], inv[:], None, ALU.mult)
+                    nc.sync.dma_start(rows[:, lo:hi], y[:])

@@ -42,25 +42,23 @@ def tile_attend_wts_topk_kernel(tc, qT, k_words, k_scales, offs, out):
             return raw
 
         nc.vector.memset(scale_pool[0:96, :], 0)
-        nc.scalar.dma_start(scale_pool[96:P, :], k_scales.bitcast(I32).rearrange("o f t -> f o t"))
+        nc.sync.dma_start(scale_pool[96:P, :], k_scales.bitcast(I32).rearrange("o f t -> f o t"))
         nc.sync.dma_start(offsets[:], offs)
         nc.sync.dma_start(word_pool[:], k_words[0].rearrange("p t b -> p (t b)").bitcast(I32))
         r00 = load_q(0, 0, P)
-        r10 = load_q(1, 0, P)
-
-        warm_in = keep.tile([P, 1], F32, name="warm_in")
-        warm_out = keep.tile([P, 1], F32, name="warm_out")
-        nc.gpsimd.memset(warm_in[:], 0.0)
-        nc.scalar.activation(warm_out[:], warm_in[:], ACT.Exp)
+        r1 = keep.tile([P, PACK, NQ], F32, name="q_raw1", align_bytes=64)
+        r1_runs = r1[:].rearrange("p (a j) w -> p a (j w)", a=2)
+        q1_runs = q_rows[1].rearrange("p (a j) w -> p a (j w)", a=2)
+        nc.sync.dma_start(r1_runs[:, :, 0 : 3 * P], q1_runs[:, :, 0 : 3 * P])
 
         k_planes = keep.tile([P, PASSES * N // 4], I32, name="k_planes", align_bytes=64)
         nc.vector.memset(k_planes[:], 0)
         scale_rows = keep.tile([P, N], U8, name="scale_rows", align_bytes=64)
         nc.vector.tensor_copy(scale_rows[:], scale_pool[:].bitcast(U8).indirect(offsets[:]))
         for q in range(4):
-            (nc.sync, nc.scalar)[q % 2].dma_start(k_planes[32 * q : 32 * q + 4, :], scale_rows[96 + 8 * q : 96 + 8 * q + 8, :].bitcast(I32))
+            nc.sync.dma_start(k_planes[32 * q : 32 * q + 4, :], scale_rows[96 + 8 * q : 96 + 8 * q + 8, :].bitcast(I32))
+        nc.sync.dma_start(r1_runs[:, :, 3 * P : 4 * P], q1_runs[:, :, 3 * P : 4 * P])
         r01 = load_q(0, P, NQ)
-        r11 = load_q(1, P, NQ)
         k_plane = [k_planes[:].bitcast(U8)[:, o * N : (o + 1) * N] for o in range(PASSES)]
 
         word_pairs = keep.tile([P, N], U32, name="word_pairs", align_bytes=64)
@@ -104,7 +102,7 @@ def tile_attend_wts_topk_kernel(tc, qT, k_words, k_scales, offs, out):
                 stop=stop,
             )
 
-        g00, g01, g10 = bf16_tile(0, 0), bf16_tile(0, 1), bf16_tile(1, 0)
+        g00, g01, g10, g11 = bf16_tile(0, 0), bf16_tile(0, 1), bf16_tile(1, 0), bf16_tile(1, 1)
         round_q(g00, r00, 0, 0, P, False)
         q00 = quantise(0, 0, g00)
         k0 = keep.tile([P, N], U16, name="k_codes0", tag="q_raw0_0", align_bytes=64)
@@ -112,31 +110,19 @@ def tile_attend_wts_topk_kernel(tc, qT, k_words, k_scales, offs, out):
             nc.vector.tensor_copy(k0[:, lo:hi], halves[:, 0, lo:hi])
             multiply(0, 0, q00, k0[:, lo:hi], lo, hi, lo == 0, False)
         k1 = part_words(1, 0, N, "grouped0_0")
-        round_q(g10, r10, 0, 0, P, False)
+        round_q(g10, r1, 0, 0, P, False)
         q10 = quantise(1, 0, g10)
         multiply(1, 0, q10, k1[:], 0, N, False, True)
-        round_q(g01, r01, 0, 0, 96, False)
-        round_q(g01, r01, 0, 96, P, True)
+        round_q(g11, r1, -P, 0, 64, False)
+        round_q(g11, r1, -P, 64, P, True)
+        round_q(g01, r01, 0, 0, 64, False)
+        round_q(g01, r01, 0, 64, P, True)
+        q11 = quantise(1, 1, g11)
+        multiply(1, 1, q11, k1[:], 0, N, True, False)
         q01 = quantise(0, 1, g01)
-        multiply(0, 1, q01, k0[:], 0, N, True, False)
-        q11 = (
-            keep.tile([P, P], U32, name="q_codes1_1", align_bytes=64),
-            keep.tile([P, P], U8, name="q_plane1_1", align_bytes=64),
-        )
-        g11 = [
-            keep.tile([P, 64, PACK], BF16, name="grouped1_1a", align_bytes=64),
-            keep.tile([P, 64, PACK], BF16, name="grouped1_1b", tag="grouped0_1", align_bytes=64),
-        ]
-        for h in range(2):
-            round_q(g11[h], r11, -64 * h, 0, 64, h == 1)
-        for h in range(2):
-            cols = slice(64 * h, 64 * h + 64)
-            nc.vector.quantize_mx(
-                out=q11[0][:, cols].bitcast(FP8X4), scales=q11[1][:, cols], in_=g11[h][:].rearrange("p w j -> p (w j)")
-            )
-        multiply(1, 1, q11, k1[:], 0, N, False, True)
+        multiply(0, 1, q01, k0[:], 0, N, False, True)
 
-        neg_max = [keep.tile([P, 1], F32, name="neg_max%d" % b, tag=("q_raw1_128", "neg_max1")[b], align_bytes=64) for b in range(QB)]
+        neg_max = [keep.tile([P, 1], F32, name="neg_max%d" % b, tag=("q_raw0_128", "neg_max1")[b], align_bytes=64) for b in range(QB)]
         row_sum = [keep.tile([P, 1], F32, name="row_sum%d" % b) for b in range(QB)]
         e = [keep.tile([P, N], F32, name="e%d" % b) for b in range(QB)]
         for b in range(QB):
@@ -146,12 +132,7 @@ def tile_attend_wts_topk_kernel(tc, qT, k_words, k_scales, offs, out):
             inv = keep.tile([P, 1], F32, name="inv%d" % b)
             nc.vector.reciprocal(inv[:], row_sum[b][:])
             rows = out[0, b * P : (b + 1) * P, :]
-            cuts = ((0, 192), (192, N)) if b == 0 else ((0, 128), (128, 320), (320, N))
-            for lo, hi in cuts:
+            for lo, hi in ((0, 192), (192, N)):
                 y = keep.tile([P, hi - lo], F32, name="y%d_%d" % (b, lo))
-                if b == 1 and lo == 0:
-                    nc.scalar.activation(y[:], e[b][:, lo:hi], ACT.Copy, scale=inv[:])
-                    nc.scalar.dma_start(rows[:, lo:hi], y[:])
-                else:
-                    nc.vector.tensor_scalar(y[:], e[b][:, lo:hi], inv[:], None, ALU.mult)
-                    nc.sync.dma_start(rows[:, lo:hi], y[:])
+                nc.vector.tensor_scalar(y[:], e[b][:, lo:hi], inv[:], None, ALU.mult)
+                nc.sync.dma_start(rows[:, lo:hi], y[:])

@@ -46,10 +46,7 @@ def tile_attend_wts_topk_kernel(tc, qT, k_words, k_scales, offs, out):
         nc.sync.dma_start(offsets[:], offs)
         nc.sync.dma_start(word_pool[:], k_words[0].rearrange("p t b -> p (t b)").bitcast(I32))
         r00 = load_q(0, 0, P)
-        r1 = keep.tile([P, PACK, NQ], F32, name="q_raw1", align_bytes=64)
-        r1_runs = r1[:].rearrange("p (a j) w -> p a (j w)", a=2)
-        q1_runs = q_rows[1].rearrange("p (a j) w -> p a (j w)", a=2)
-        nc.sync.dma_start(r1_runs[:, :, 0 : 3 * P], q1_runs[:, :, 0 : 3 * P])
+        r10 = load_q(1, 0, P)
 
         k_planes = keep.tile([P, PASSES * N // 4], I32, name="k_planes", align_bytes=64)
         nc.vector.memset(k_planes[:], 0)
@@ -57,8 +54,8 @@ def tile_attend_wts_topk_kernel(tc, qT, k_words, k_scales, offs, out):
         nc.vector.tensor_copy(scale_rows[:], scale_pool[:].bitcast(U8).indirect(offsets[:]))
         for q in range(4):
             nc.sync.dma_start(k_planes[32 * q : 32 * q + 4, :], scale_rows[96 + 8 * q : 96 + 8 * q + 8, :].bitcast(I32))
-        nc.sync.dma_start(r1_runs[:, :, 3 * P : 4 * P], q1_runs[:, :, 3 * P : 4 * P])
         r01 = load_q(0, P, NQ)
+        r11 = load_q(1, P, NQ)
         k_plane = [k_planes[:].bitcast(U8)[:, o * N : (o + 1) * N] for o in range(PASSES)]
 
         word_pairs = keep.tile([P, N], U32, name="word_pairs", align_bytes=64)
@@ -75,10 +72,13 @@ def tile_attend_wts_topk_kernel(tc, qT, k_words, k_scales, offs, out):
         def bf16_tile(o, b):
             return keep.tile([P, P, PACK], BF16, name="grouped%d_%d" % (o, b), align_bytes=64)
 
-        def round_q(grouped, raw, first, lo, hi, on_vector):
+        def round_q(grouped, raw, first, lo, hi, on_vector, on_gpsimd=False):
             dst = grouped[:, lo:hi, :].rearrange("p (c i) t -> p c t i", i=4)
             src = raw[:, :, lo - first : hi - first].rearrange("p t (c i) -> p c t i", i=4)
-            if on_vector:
+            if on_gpsimd:
+                stepped = raw[:, :, lo - first : hi - first].rearrange("p t w -> p w t")
+                nc.gpsimd.tensor_scalar(grouped[:, lo:hi, :], stepped, 1.0, 0.0, ALU.mult, ALU.add)
+            elif on_vector:
                 nc.vector.tensor_copy(dst, src)
             else:
                 nc.scalar.activation(dst, src, ACT.Copy)
@@ -103,26 +103,27 @@ def tile_attend_wts_topk_kernel(tc, qT, k_words, k_scales, offs, out):
             )
 
         g00, g01, g10, g11 = bf16_tile(0, 0), bf16_tile(0, 1), bf16_tile(1, 0), bf16_tile(1, 1)
-        round_q(g00, r00, 0, 0, P, False)
+        round_q(g00, r00, 0, 0, 80, False)
+        round_q(g00, r00, 0, 80, P, False, True)
         q00 = quantise(0, 0, g00)
         k0 = keep.tile([P, N], U16, name="k_codes0", tag="q_raw0_0", align_bytes=64)
         for lo, hi in ((0, N // 2), (N // 2, N)):
             nc.vector.tensor_copy(k0[:, lo:hi], halves[:, 0, lo:hi])
             multiply(0, 0, q00, k0[:, lo:hi], lo, hi, lo == 0, False)
         k1 = part_words(1, 0, N, "grouped0_0")
-        round_q(g10, r1, 0, 0, P, False)
+        round_q(g10, r10, 0, 0, P, False)
         q10 = quantise(1, 0, g10)
         multiply(1, 0, q10, k1[:], 0, N, False, True)
-        round_q(g11, r1, -P, 0, 64, False)
-        round_q(g11, r1, -P, 64, P, True)
-        round_q(g01, r01, 0, 0, 64, False)
-        round_q(g01, r01, 0, 64, P, True)
-        q11 = quantise(1, 1, g11)
-        multiply(1, 1, q11, k1[:], 0, N, True, False)
+        round_q(g01, r01, 0, 0, 104, False)
+        round_q(g01, r01, 0, 104, P, True)
+        round_q(g11, r11, 0, 0, 48, False)
+        round_q(g11, r11, 0, 48, P, True)
         q01 = quantise(0, 1, g01)
-        multiply(0, 1, q01, k0[:], 0, N, False, True)
+        multiply(0, 1, q01, k0[:], 0, N, True, False)
+        q11 = quantise(1, 1, g11)
+        multiply(1, 1, q11, k1[:], 0, N, False, True)
 
-        neg_max = [keep.tile([P, 1], F32, name="neg_max%d" % b, tag=("q_raw0_128", "neg_max1")[b], align_bytes=64) for b in range(QB)]
+        neg_max = [keep.tile([P, 1], F32, name="neg_max%d" % b, tag=("grouped1_1", "neg_max1")[b], align_bytes=64) for b in range(QB)]
         row_sum = [keep.tile([P, 1], F32, name="row_sum%d" % b) for b in range(QB)]
         e = [keep.tile([P, N], F32, name="e%d" % b) for b in range(QB)]
         for b in range(QB):

@@ -102,7 +102,7 @@ def tile_attend_wts_topk_kernel(tc, qT, k_words, k_scales, offs, out):
                 stop=stop,
             )
 
-        g00, g01, g10, g11 = bf16_tile(0, 0), bf16_tile(0, 1), bf16_tile(1, 0), bf16_tile(1, 1)
+        g00, g01, g10 = bf16_tile(0, 0), bf16_tile(0, 1), bf16_tile(1, 0)
         round_q(g00, r00, 0, 0, 80, False)
         round_q(g00, r00, 0, 80, P, False, True)
         q00 = quantise(0, 0, g00)
@@ -114,16 +114,28 @@ def tile_attend_wts_topk_kernel(tc, qT, k_words, k_scales, offs, out):
         round_q(g10, r10, 0, 0, P, False)
         q10 = quantise(1, 0, g10)
         multiply(1, 0, q10, k1[:], 0, N, False, True)
-        round_q(g01, r01, 0, 0, 104, False)
-        round_q(g01, r01, 0, 104, P, True)
-        round_q(g11, r11, 0, 0, 48, False)
-        round_q(g11, r11, 0, 48, P, True)
+        round_q(g01, r01, 0, 0, 80, False)
+        round_q(g01, r01, 0, 80, P, True)
         q01 = quantise(0, 1, g01)
         multiply(0, 1, q01, k0[:], 0, N, True, False)
-        q11 = quantise(1, 1, g11)
+        q11 = (
+            keep.tile([P, P], U32, name="q_codes1_1", align_bytes=64),
+            keep.tile([P, P], U8, name="q_plane1_1", align_bytes=64),
+        )
+        g11 = [
+            keep.tile([P, 64, PACK], BF16, name="grouped1_1a", align_bytes=64),
+            keep.tile([P, 64, PACK], BF16, name="grouped1_1b", tag="grouped0_1", align_bytes=64),
+        ]
+        for h in range(2):
+            round_q(g11[h], r11, -64 * h, 0, 64, h == 1)
+        for h in range(2):
+            cols = slice(64 * h, 64 * h + 64)
+            nc.vector.quantize_mx(
+                out=q11[0][:, cols].bitcast(FP8X4), scales=q11[1][:, cols], in_=g11[h][:].rearrange("p w j -> p (w j)")
+            )
         multiply(1, 1, q11, k1[:], 0, N, False, True)
 
-        neg_max = [keep.tile([P, 1], F32, name="neg_max%d" % b, tag=("grouped1_1", "neg_max1")[b], align_bytes=64) for b in range(QB)]
+        neg_max = [keep.tile([P, 1], F32, name="neg_max%d" % b, tag=("q_raw1_128", "neg_max1")[b], align_bytes=64) for b in range(QB)]
         row_sum = [keep.tile([P, 1], F32, name="row_sum%d" % b) for b in range(QB)]
         e = [keep.tile([P, N], F32, name="e%d" % b) for b in range(QB)]
         for b in range(QB):

@@ -124,7 +124,7 @@ def tile_attend_wts_topk_kernel(tc, qT, k_words, k_scales, offs, out):
         )
         g11 = [
             keep.tile([P, 64, PACK], BF16, name="grouped1_1a", align_bytes=64),
-            keep.tile([P, 64, PACK], BF16, name="grouped1_1b", tag="grouped0_1", align_bytes=64),
+            keep.tile([P, 64, PACK], BF16, name="grouped1_1b", tag="q_raw0_128", align_bytes=64),
         ]
         for h in range(2):
             round_q(g11[h], r11, -64 * h, 0, 64, h == 1)

@@ -22,6 +22,11 @@ PACK = 4
 K_PASS = P * PACK
 PASSES = D // K_PASS
 QB = NQ // P
+SCALAR_FIRST = 80
+SCALAR_THIRD = 56
+HALF = P // 2
+SCALAR_LAST = 24
+FIRST_STORE = 192
 
 
 def tile_attend_wts_topk_kernel(tc, qT, k_words, k_scales, offs, out):
@@ -30,15 +35,17 @@ def tile_attend_wts_topk_kernel(tc, qT, k_words, k_scales, offs, out):
         keep = ctx.enter_context(tc.tile_pool(name="keep", bufs=1))
         psum = ctx.enter_context(tc.psum_pool(name="psum", bufs=1))
 
-        offsets = keep.tile([P, N // 16], U16, name="offsets")
-        scale_pool = keep.tile([P, T // 4], I32, name="scale_pool", align_bytes=64)
-        word_pool = keep.tile([P, T], I32, name="word_pool", align_bytes=64)
-        q_rows = [qT[0, o * K_PASS : (o + 1) * K_PASS, :].rearrange("(p j) w -> p j w", j=PACK) for o in range(PASSES)]
+        def sbuf(shape, dtype, name, tag=None):
+            return keep.tile(shape, dtype, name=name, tag=tag or name, align_bytes=64)
 
-        def load_q(o, lo, hi, queue=nc.sync, tag=None):
-            name = "q_raw%d_%d" % (o, lo)
-            raw = keep.tile([P, PACK, hi - lo], F32, name=name, tag=tag or name, align_bytes=64)
-            queue.dma_start(raw[:], q_rows[o][:, :, lo:hi])
+        offsets = keep.tile([P, N // 16], U16, name="offsets")
+        scale_pool = sbuf([P, T // 4], I32, "scale_pool")
+        word_pool = sbuf([P, T], I32, "word_pool")
+
+        def load_q(o, lo, hi):
+            raw = sbuf([P, PACK, hi - lo], F32, "q_raw%d_%d" % (o, lo))
+            rows = qT[0, o * K_PASS : (o + 1) * K_PASS, lo:hi]
+            nc.sync.dma_start(raw[:], rows.rearrange("(p j) w -> p j w", j=PACK))
             return raw
 
         nc.vector.memset(scale_pool[0:96, :], 0)
@@ -48,104 +55,90 @@ def tile_attend_wts_topk_kernel(tc, qT, k_words, k_scales, offs, out):
         r00 = load_q(0, 0, P)
         r10 = load_q(1, 0, P)
 
-        k_planes = keep.tile([P, PASSES * N // 4], I32, name="k_planes", align_bytes=64)
+        k_planes = sbuf([P, PASSES * N // 4], I32, "k_planes")
         nc.vector.memset(k_planes[:], 0)
-        scale_rows = keep.tile([P, N], U8, name="scale_rows", align_bytes=64)
+        scale_rows = sbuf([P, N], U8, "scale_rows")
         nc.vector.tensor_copy(scale_rows[:], scale_pool[:].bitcast(U8).indirect(offsets[:]))
         for q in range(4):
             nc.sync.dma_start(k_planes[32 * q : 32 * q + 4, :], scale_rows[96 + 8 * q : 96 + 8 * q + 8, :].bitcast(I32))
         r01 = load_q(0, P, NQ)
-        r11 = load_q(1, P, NQ)
+        r11 = [load_q(1, P + HALF * h, P + HALF * (h + 1)) for h in range(2)]
         k_plane = [k_planes[:].bitcast(U8)[:, o * N : (o + 1) * N] for o in range(PASSES)]
 
-        word_pairs = keep.tile([P, N], U32, name="word_pairs", align_bytes=64)
+        word_pairs = sbuf([P, N], U32, "word_pairs")
         nc.vector.tensor_copy(word_pairs[:], word_pool[:].bitcast(U32).indirect(offsets[:]))
         halves = word_pairs[:].bitcast(U16).rearrange("p (n o) -> p o n", o=PASSES)
         scores = [psum.tile([P, N], F32, name="scores%d" % b) for b in range(QB)]
 
-        def part_words(o, lo, hi, tag=None):
-            name = "k_codes%d_%d" % (o, lo)
-            codes = keep.tile([P, hi - lo], U16, name=name, tag=tag or name, align_bytes=64)
-            nc.vector.tensor_copy(codes[:], halves[:, o, lo:hi])
-            return codes
+        def walk(grouped, raw, lo, hi, at=0):
+            dst = grouped[:, lo - at : hi - at, :].rearrange("p (c i) t -> p c t i", i=4)
+            src = raw[:, :, lo:hi].rearrange("p t (c i) -> p c t i", i=4)
+            return dst, src
 
-        def bf16_tile(o, b):
-            return keep.tile([P, P, PACK], BF16, name="grouped%d_%d" % (o, b), align_bytes=64)
+        def mx_tiles(o, b):
+            return sbuf([P, P], U32, "q_codes%d%d" % (o, b)), sbuf([P, P], U8, "q_plane%d%d" % (o, b))
 
-        def round_q(grouped, raw, first, lo, hi, on_vector, on_gpsimd=False):
-            dst = grouped[:, lo:hi, :].rearrange("p (c i) t -> p c t i", i=4)
-            src = raw[:, :, lo - first : hi - first].rearrange("p t (c i) -> p c t i", i=4)
-            if on_gpsimd:
-                stepped = raw[:, :, lo - first : hi - first].rearrange("p t w -> p w t")
-                nc.gpsimd.tensor_scalar(grouped[:, lo:hi, :], stepped, 1.0, 0.0, ALU.mult, ALU.add)
-            elif on_vector:
-                nc.vector.tensor_copy(dst, src)
-            else:
-                nc.scalar.activation(dst, src, ACT.Copy)
-
-        def quantise(o, b, grouped):
-            q_codes = keep.tile([P, P], U32, name="q_codes%d_%d" % (o, b), align_bytes=64)
-            q_plane = keep.tile([P, P], U8, name="q_plane%d_%d" % (o, b), align_bytes=64)
+        def quantise(q, grouped, lo, hi):
             nc.vector.quantize_mx(
-                out=q_codes[:].bitcast(FP8X4), scales=q_plane[:], in_=grouped[:].rearrange("p w j -> p (w j)")
+                out=q[0][:, lo:hi].bitcast(FP8X4), scales=q[1][:, lo:hi], in_=grouped[:].rearrange("p w j -> p (w j)")
             )
-            return q_codes, q_plane
 
         def multiply(o, b, q, k_codes, lo, hi, start, stop):
             nc.tensor.matmul_mx(
                 out=scores[b][:, lo:hi],
                 lhsT=q[0][:].bitcast(FP8X4),
                 lhsT_scale=q[1][:],
-                rhs=k_codes.bitcast(FP4X4),
+                rhs=k_codes[:, lo:hi].bitcast(FP4X4),
                 rhs_scale=k_plane[o][:, lo:hi],
                 start=start,
                 stop=stop,
             )
 
-        g00, g01, g10 = bf16_tile(0, 0), bf16_tile(0, 1), bf16_tile(1, 0)
-        round_q(g00, r00, 0, 0, 80, False)
-        round_q(g00, r00, 0, 80, P, False, True)
-        q00 = quantise(0, 0, g00)
-        k0 = keep.tile([P, N], U16, name="k_codes0", tag="q_raw0_0", align_bytes=64)
+        g00 = sbuf([P, P, PACK], BF16, "grouped00")
+        nc.scalar.activation(*walk(g00, r00, 0, SCALAR_FIRST), ACT.Copy)
+        stepped = r00[:, :, SCALAR_FIRST:P].rearrange("p t w -> p w t")
+        nc.gpsimd.tensor_scalar(g00[:, SCALAR_FIRST:P, :], stepped, 1.0, 0.0, ALU.mult, ALU.add)
+        q00 = mx_tiles(0, 0)
+        quantise(q00, g00, 0, P)
+        k0 = sbuf([P, N], U16, "k_codes0", tag="q_raw0_0")
         for lo, hi in ((0, N // 2), (N // 2, N)):
             nc.vector.tensor_copy(k0[:, lo:hi], halves[:, 0, lo:hi])
-            multiply(0, 0, q00, k0[:, lo:hi], lo, hi, lo == 0, False)
-        k1 = part_words(1, 0, N, "grouped0_0")
-        round_q(g10, r10, 0, 0, P, False)
-        q10 = quantise(1, 0, g10)
-        multiply(1, 0, q10, k1[:], 0, N, False, True)
-        round_q(g01, r01, 0, 0, 80, False)
-        round_q(g01, r01, 0, 80, P, True)
-        q01 = quantise(0, 1, g01)
-        multiply(0, 1, q01, k0[:], 0, N, True, False)
-        q11 = (
-            keep.tile([P, P], U32, name="q_codes1_1", align_bytes=64),
-            keep.tile([P, P], U8, name="q_plane1_1", align_bytes=64),
-        )
-        g11 = [
-            keep.tile([P, 64, PACK], BF16, name="grouped1_1a", align_bytes=64),
-            keep.tile([P, 64, PACK], BF16, name="grouped1_1b", tag="q_raw0_128", align_bytes=64),
-        ]
-        for h in range(2):
-            round_q(g11[h], r11, -64 * h, 0, 64, h == 1)
-        for h in range(2):
-            cols = slice(64 * h, 64 * h + 64)
-            nc.vector.quantize_mx(
-                out=q11[0][:, cols].bitcast(FP8X4), scales=q11[1][:, cols], in_=g11[h][:].rearrange("p w j -> p (w j)")
-            )
-        multiply(1, 1, q11, k1[:], 0, N, False, True)
+            multiply(0, 0, q00, k0, lo, hi, lo == 0, False)
+        k1 = sbuf([P, N], U16, "k_codes1", tag="grouped00")
+        nc.vector.tensor_copy(k1[:], halves[:, 1, :])
+        g10 = sbuf([P, P, PACK], BF16, "grouped10")
+        nc.scalar.activation(*walk(g10, r10, 0, P), ACT.Copy)
+        q10 = mx_tiles(1, 0)
+        quantise(q10, g10, 0, P)
+        multiply(1, 0, q10, k1, 0, N, False, True)
 
-        neg_max = [keep.tile([P, 1], F32, name="neg_max%d" % b, tag=("q_raw1_128", "neg_max1")[b], align_bytes=64) for b in range(QB)]
-        row_sum = [keep.tile([P, 1], F32, name="row_sum%d" % b) for b in range(QB)]
-        e = [keep.tile([P, N], F32, name="e%d" % b) for b in range(QB)]
+        g01 = sbuf([P, P, PACK], BF16, "grouped01")
+        nc.scalar.activation(*walk(g01, r01, 0, SCALAR_THIRD), ACT.Copy)
+        nc.vector.tensor_copy(*walk(g01, r01, SCALAR_THIRD, P))
+        q01 = mx_tiles(0, 1)
+        quantise(q01, g01, 0, P)
+        multiply(0, 1, q01, k0, 0, N, True, False)
+
+        q11 = mx_tiles(1, 1)
+        g11 = [sbuf([P, HALF, PACK], BF16, "grouped11a"), sbuf([P, HALF, PACK], BF16, "grouped11b", tag="q_raw0_128")]
+        nc.scalar.activation(*walk(g11[0], r11[0], 0, HALF), ACT.Copy)
+        nc.scalar.activation(*walk(g11[1], r11[1], 0, SCALAR_LAST), ACT.Copy)
+        nc.vector.tensor_copy(*walk(g11[1], r11[1], SCALAR_LAST, HALF))
+        for h in range(2):
+            quantise(q11, g11[h], HALF * h, HALF * (h + 1))
+        multiply(1, 1, q11, k1, 0, N, False, True)
+
+        neg_max = [sbuf([P, 1], F32, "neg_max0", tag="q_raw1_192"), sbuf([P, 1], F32, "neg_max1")]
+        row_sum = [sbuf([P, 1], F32, "row_sum%d" % b) for b in range(QB)]
+        e = [sbuf([P, N], F32, "e%d" % b) for b in range(QB)]
         for b in range(QB):
             nc.vector.tensor_reduce(neg_max[b][:], scores[b][:], AX.X, ALU.max, negate=True)
             nc.scalar.activation(e[b][:], scores[b][:], ACT.Exp, bias=neg_max[b][:], scale=1.0, accum_out=row_sum[b][:])
         for b in range(QB):
-            inv = keep.tile([P, 1], F32, name="inv%d" % b)
+            inv = sbuf([P, 1], F32, "inv%d" % b)
             nc.vector.reciprocal(inv[:], row_sum[b][:])
             rows = out[0, b * P : (b + 1) * P, :]
-            for lo, hi in ((0, 192), (192, N)):
-                y = keep.tile([P, hi - lo], F32, name="y%d_%d" % (b, lo))
+            for lo, hi in ((0, FIRST_STORE), (FIRST_STORE, N)):
+                y = sbuf([P, hi - lo], F32, "y%d_%d" % (b, lo))
                 nc.vector.tensor_scalar(y[:], e[b][:, lo:hi], inv[:], None, ALU.mult)
                 nc.sync.dma_start(rows[:, lo:hi], y[:])

@@ -23,6 +23,7 @@ K_PASS = P * PACK
 PASSES = D // K_PASS
 QB = NQ // P
 SCALAR_FIRST = 80
+SCALAR_SECOND = 96
 SCALAR_THIRD = 56
 HALF = P // 2
 SCALAR_LAST = 24
@@ -104,13 +105,16 @@ def tile_attend_wts_topk_kernel(tc, qT, k_words, k_scales, offs, out):
         for lo, hi in ((0, N // 2), (N // 2, N)):
             nc.vector.tensor_copy(k0[:, lo:hi], halves[:, 0, lo:hi])
             multiply(0, 0, q00, k0, lo, hi, lo == 0, False)
-        k1 = sbuf([P, N], U16, "k_codes1", tag="grouped00")
-        nc.vector.tensor_copy(k1[:], halves[:, 1, :])
         g10 = sbuf([P, P, PACK], BF16, "grouped10")
-        nc.scalar.activation(*walk(g10, r10, 0, P), ACT.Copy)
+        nc.scalar.activation(*walk(g10, r10, 0, SCALAR_SECOND), ACT.Copy)
+        nc.vector.tensor_copy(*walk(g10, r10, SCALAR_SECOND, P))
+        k1 = sbuf([P, N], U16, "k_codes1", tag="grouped00")
+        nc.vector.tensor_copy(k1[:, 0 : N // 2], halves[:, 1, 0 : N // 2])
         q10 = mx_tiles(1, 0)
         quantise(q10, g10, 0, P)
-        multiply(1, 0, q10, k1, 0, N, False, True)
+        multiply(1, 0, q10, k1, 0, N // 2, False, False)
+        nc.vector.tensor_copy(k1[:, N // 2 : N], halves[:, 1, N // 2 : N])
+        multiply(1, 0, q10, k1, N // 2, N, False, True)
 
         g01 = sbuf([P, P, PACK], BF16, "grouped01")
         nc.scalar.activation(*walk(g01, r01, 0, SCALAR_THIRD), ACT.Copy)

from contextlib import ExitStack

import concourse.mybir as mybir

T, D, NQ, N = 2048, 1024, 256, 512
FLOPS = 2 * D * NQ * N

F32 = mybir.dt.float32
BF16 = mybir.dt.bfloat16
I32 = mybir.dt.int32
U32 = mybir.dt.uint32
U16 = mybir.dt.uint16
U8 = mybir.dt.uint8
FP8X4 = mybir.dt.float8_e4m3fn_x4
FP4X4 = mybir.dt.float4_e2m1fn_x4
ACT = mybir.ActivationFunctionType
ALU = mybir.AluOpType
AX = mybir.AxisListType

P = 128
PACK = 4
K_PASS = P * PACK
PASSES = D // K_PASS
QB = NQ // P
SCALAR_FIRST = 80
SCALAR_SECOND = 96
SCALAR_THIRD = 56
HALF = P // 2
SCALAR_LAST = 24
FIRST_STORE = 192


def tile_attend_wts_topk_kernel(tc, qT, k_words, k_scales, offs, out):
    nc = tc.nc
    with ExitStack() as ctx:
        keep = ctx.enter_context(tc.tile_pool(name="keep", bufs=1))
        psum = ctx.enter_context(tc.psum_pool(name="psum", bufs=1))

        def sbuf(shape, dtype, name, tag=None):
            return keep.tile(shape, dtype, name=name, tag=tag or name, align_bytes=64)

        offsets = keep.tile([P, N // 16], U16, name="offsets")
        scale_pool = sbuf([P, T // 4], I32, "scale_pool")
        word_pool = sbuf([P, T], I32, "word_pool")

        def load_q(o, lo, hi):
            raw = sbuf([P, PACK, hi - lo], F32, "q_raw%d_%d" % (o, lo))
            rows = qT[0, o * K_PASS : (o + 1) * K_PASS, lo:hi]
            nc.sync.dma_start(raw[:], rows.rearrange("(p j) w -> p j w", j=PACK))
            return raw

        nc.vector.memset(scale_pool[0:96, :], 0)
        nc.sync.dma_start(scale_pool[96:P, :], k_scales.bitcast(I32).rearrange("o f t -> f o t"))
        nc.sync.dma_start(offsets[:], offs)
        nc.sync.dma_start(word_pool[:], k_words[0].rearrange("p t b -> p (t b)").bitcast(I32))
        r00 = load_q(0, 0, P)
        r10 = load_q(1, 0, P)

        k_planes = sbuf([P, PASSES * N // 4], I32, "k_planes")
        nc.vector.memset(k_planes[:], 0)
        scale_rows = sbuf([P, N], U8, "scale_rows")
        nc.vector.tensor_copy(scale_rows[:], scale_pool[:].bitcast(U8).indirect(offsets[:]))
        for q in range(4):
            nc.sync.dma_start(k_planes[32 * q : 32 * q + 4, :], scale_rows[96 + 8 * q : 96 + 8 * q + 8, :].bitcast(I32))
        r01 = load_q(0, P, NQ)
        r11 = [load_q(1, P + HALF * h, P + HALF * (h + 1)) for h in range(2)]
        k_plane = [k_planes[:].bitcast(U8)[:, o * N : (o + 1) * N] for o in range(PASSES)]

        word_pairs = sbuf([P, N], U32, "word_pairs")
        nc.vector.tensor_copy(word_pairs[:], word_pool[:].bitcast(U32).indirect(offsets[:]))
        halves = word_pairs[:].bitcast(U16).rearrange("p (n o) -> p o n", o=PASSES)
        scores = [psum.tile([P, N], F32, name="scores%d" % b) for b in range(QB)]

        def walk(grouped, raw, lo, hi, at=0):
            dst = grouped[:, lo - at : hi - at, :].rearrange("p (c i) t -> p c t i", i=4)
            src = raw[:, :, lo:hi].rearrange("p t (c i) -> p c t i", i=4)
            return dst, src

        def mx_tiles(o, b):
            return sbuf([P, P], U32, "q_codes%d%d" % (o, b)), sbuf([P, P], U8, "q_plane%d%d" % (o, b))

        def quantise(q, grouped, lo, hi):
            nc.vector.quantize_mx(
                out=q[0][:, lo:hi].bitcast(FP8X4), scales=q[1][:, lo:hi], in_=grouped[:].rearrange("p w j -> p (w j)")
            )

        def multiply(o, b, q, k_codes, lo, hi, start, stop):
            nc.tensor.matmul_mx(
                out=scores[b][:, lo:hi],
                lhsT=q[0][:].bitcast(FP8X4),
                lhsT_scale=q[1][:],
                rhs=k_codes[:, lo:hi].bitcast(FP4X4),
                rhs_scale=k_plane[o][:, lo:hi],
                start=start,
                stop=stop,
            )

        g00 = sbuf([P, P, PACK], BF16, "grouped00")
        nc.scalar.activation(*walk(g00, r00, 0, SCALAR_FIRST), ACT.Copy)
        stepped = r00[:, :, SCALAR_FIRST:P].rearrange("p t w -> p w t")
        nc.gpsimd.tensor_scalar(g00[:, SCALAR_FIRST:P, :], stepped, 1.0, 0.0, ALU.mult, ALU.add)
        q00 = mx_tiles(0, 0)
        quantise(q00, g00, 0, P)
        k0 = sbuf([P, N], U16, "k_codes0", tag="q_raw0_0")
        for lo, hi in ((0, N // 2), (N // 2, N)):
            nc.vector.tensor_copy(k0[:, lo:hi], halves[:, 0, lo:hi])
            multiply(0, 0, q00, k0, lo, hi, lo == 0, False)
        g10 = sbuf([P, P, PACK], BF16, "grouped10")
        nc.scalar.activation(*walk(g10, r10, 0, SCALAR_SECOND), ACT.Copy)
        nc.vector.tensor_copy(*walk(g10, r10, SCALAR_SECOND, P))
        k1 = sbuf([P, N], U16, "k_codes1", tag="grouped00")
        nc.vector.tensor_copy(k1[:, 0 : N // 2], halves[:, 1, 0 : N // 2])
        q10 = mx_tiles(1, 0)
        quantise(q10, g10, 0, P)
        multiply(1, 0, q10, k1, 0, N // 2, False, False)
        nc.vector.tensor_copy(k1[:, N // 2 : N], halves[:, 1, N // 2 : N])
        multiply(1, 0, q10, k1, N // 2, N, False, True)

        g01 = sbuf([P, P, PACK], BF16, "grouped01")
        nc.scalar.activation(*walk(g01, r01, 0, SCALAR_THIRD), ACT.Copy)
        nc.vector.tensor_copy(*walk(g01, r01, SCALAR_THIRD, P))
        q01 = mx_tiles(0, 1)
        quantise(q01, g01, 0, P)
        multiply(0, 1, q01, k0, 0, N, True, False)

        q11 = mx_tiles(1, 1)
        g11 = [sbuf([P, HALF, PACK], BF16, "grouped11a"), sbuf([P, HALF, PACK], BF16, "grouped11b", tag="q_raw0_128")]
        nc.scalar.activation(*walk(g11[0], r11[0], 0, HALF), ACT.Copy)
        nc.scalar.activation(*walk(g11[1], r11[1], 0, SCALAR_LAST), ACT.Copy)
        nc.vector.tensor_copy(*walk(g11[1], r11[1], SCALAR_LAST, HALF))
        for h in range(2):
            quantise(q11, g11[h], HALF * h, HALF * (h + 1))
        multiply(1, 1, q11, k1, 0, N, False, True)

        neg_max = [sbuf([P, 1], F32, "neg_max0", tag="q_raw1_192"), sbuf([P, 1], F32, "neg_max1")]
        row_sum = [sbuf([P, 1], F32, "row_sum%d" % b) for b in range(QB)]
        e = [sbuf([P, N], F32, "e%d" % b) for b in range(QB)]
        for b in range(QB):
            nc.vector.tensor_reduce(neg_max[b][:], scores[b][:], AX.X, ALU.max, negate=True)
            nc.scalar.activation(e[b][:], scores[b][:], ACT.Exp, bias=neg_max[b][:], scale=1.0, accum_out=row_sum[b][:])
        for b in range(QB):
            inv = sbuf([P, 1], F32, "inv%d" % b)
            nc.vector.reciprocal(inv[:], row_sum[b][:])
            rows = out[0, b * P : (b + 1) * P, :]
            for lo, hi in ((0, FIRST_STORE), (FIRST_STORE, N)):
                y = sbuf([P, hi - lo], F32, "y%d_%d" % (b, lo))
                nc.vector.tensor_scalar(y[:], e[b][:, lo:hi], inv[:], None, ALU.mult)
                nc.sync.dma_start(rows[:, lo:hi], y[:])
